import numpy as np, ml_dtypes
CORES = [40,41,42,43,44,45,46,47]
N = 8
BF = ml_dtypes.bfloat16
def gentries(a):
    return np.ascontiguousarray(a.reshape(8, 16, -1).transpose(0, 2, 1)).reshape(8, -1)
def gtable(e):
    e = np.asarray(e); return np.ascontiguousarray(e.reshape(8, -1, 16).transpose(0, 2, 1)).reshape(128, -1).astype(np.int32)
V, R = 2048, 8
def family(rng, sizes, depth, pool, mix, fall=None):
    key = np.tile(np.arange(V), (N, 1)); lev = np.zeros(V, np.int64); comp = np.zeros(V, np.int64); via = [-1] * V; o = rng.permutation(V); a = 0
    for i in range(len(sizes)):
        s, D = int(sizes[i]), int(depth[i]); m = o[a:a + s]; a += s; comp[m] = i
        if s == 1: continue
        root = int(np.min(m)); m = m[m != root]; l = np.concatenate([np.arange(1, D + 1), rng.integers(1, D + 1, s - 1 - D)])
        if fall is not None and fall[i]: m = np.sort(m)[::-1]; l = np.sort(l)
        lev[m] = l
        at = [[root]] + [[] for k in range(D)]
        for c, k in zip(m.tolist(), l.tolist()): at[k].append(c)
        for k in range(1, D + 1):
            for c in at[k]:
                p = at[k - 1][int(rng.integers(len(at[k - 1])))]; w = [q for q in pool if q != via[p]]; q = w[int(rng.integers(len(w)))]
                key[q, c] = key[q, p]; via[c] = q
    for q in range(N if mix > 0 else 0):
        h = np.flatnonzero(key[q] == np.arange(V)); t = comp[h] * (R + 1) + lev[h]; keep = rng.random(h.size) >= mix
        hk, tk = h[keep], t[keep]; s = np.argsort(tk, kind="stable"); hk, tk = hk[s], tk[s]
        lo = np.searchsorted(tk, t, "left"); n = np.searchsorted(tk, t, "right") - lo; z = ~keep & (n > 0)
        to = h + 0; to[z] = hk[lo[z] + (rng.random(np.count_nonzero(z)) * n[z]).astype(np.int64)]
        jump = np.arange(V); jump[h] = to; key[q] = jump[key[q]]
    return key
def lay(rng, key, way):
    if way == 0: o = np.lexsort((rng.random(V), rng.permutation(V)[key]))
    elif way == 1: o = np.lexsort((np.arange(V), key))
    else: o = np.lexsort((-np.arange(V), -key))
    k = key[o]; s = np.ones(V, np.int64); s[1:] = k[1:] != k[:-1]
    e = np.append(np.flatnonzero(s)[1:], V) - 1; last = np.zeros(V, np.int64); last[o] = e[np.add.accumulate(s) - 1]
    return [o, s, last]
def pack(rng, keys, ways):
    a = np.array([[lay(rng, keys[g][q], ways[q, g]) for g in range(8)] for q in range(N)])
    return {"pm": np.stack([gtable(u) for u in a[:, :, 0]]), "en": np.stack([gtable(u) for u in a[:, :, 2]]), "st": np.ascontiguousarray(a[:, :, 1]).astype(np.int32)}
def depths(rng, s):
    top = np.minimum(R, s - 1); D = np.where(top > 0, 1 + (rng.random(s.size) * top).astype(np.int64), 0); i = np.argmax(s); D[i] = top[i]; return D
def some(rng):
    out = []
    for n in rng.choice(np.arange(6, 41), 8, replace=False):
        c = np.sort(rng.choice(V - 1, int(n) - 1, replace=False)) + 1; s = np.diff(np.concatenate([[0], c, [V]]))
        out.append(family(rng, s, depths(rng, s), list(range(N)), rng.choice([0.0, 0.05, 0.15])))
    return out
def setup_inputs(rng):
    return pack(rng, some(rng), np.zeros((N, 8), np.int64))
def setup_inputs_deep(rng):
    few = rng.permutation(8)[:4]; n = rng.choice(np.arange(V // (2 * (R + 1)), V // (R + 1) + 1), 8, replace=False); keys = []
    for g in range(8):
        m = int(n[g]); s = [R + 1] * m + [1] * (V - m * (R + 1)); pool = rng.permutation(N)[:2].tolist() if g in few else list(range(N))
        keys.append(family(rng, s, [R] * m + [0] * (V - m * (R + 1)), pool, 0.0, np.arange(len(s)) % 2 == 0))
    return pack(rng, keys, np.zeros((N, 8), np.int64))
def setup_inputs_ends(rng):
    keys = some(rng); w = rng.permutation(8); one = np.tile(np.arange(V), (N, 1))
    keys[w[0]][rng.integers(N)] = 0
    keys[w[1]] = one + 0
    keys[w[2]] = np.tile(rng.integers(0, 30, V), (N, 1))
    keys[w[3]] = one + 0; keys[w[3]][rng.integers(N)] = rng.integers(0, 3, V)
    x = np.concatenate([[0], 1 + rng.choice(V - 2, R - 1, replace=False), [V - 1]]); k = one + 0; ab = rng.permutation(N)[:2]
    for i in range(R): k[ab[i % 2], x[i + 1]] = x[i]
    keys[w[4]] = k
    return pack(rng, keys, np.zeros((N, 8), np.int64))
def setup_inputs_order(rng):
    return pack(rng, some(rng), rng.integers(1, 3, (N, 8)))
def setup_inputs_spread(rng):
    keys = []; half = int(rng.integers(8))
    for g in range(8):
        s = [1] * (V // 2 if g == half else 0); left = V - len(s)
        while left > 0:
            t = max(1, int(left * (0.3 + 0.4 * rng.random()))); s.append(t); left -= t
        s = np.array(s); keys.append(family(rng, s, depths(rng, s), list(range(N)) + [int(rng.integers(N))] * (3 * N), rng.choice([0.0, 0.3, 0.8])))
    return pack(rng, keys, np.zeros((N, 8), np.int64))
def hop(p, st, L):
    g = np.arange(8)[:, None]; M = L
    for q in range(N):
        s = st[q].reshape(-1); m = np.minimum.reduceat(L[g, p[q]].reshape(-1), np.flatnonzero(s))
        u = np.empty_like(L); u[g, p[q]] = m[np.add.accumulate(s) - 1].reshape(8, V); M = np.minimum(M, u)
    return M
def check_inputs(d):
    p = np.stack([gentries(a) for a in d["pm"]]); e = np.stack([gentries(a) for a in d["en"]]); s = d["st"]
    if not (np.sort(p, -1) == np.arange(V)).all(): return ["pm: every vertex once"]
    if not (((s == 0) | (s == 1)).all() and (s[:, :, 0] == 1).all()): return ["st: 0 and 1, beginning with 1"]
    bad = []; t = s.reshape(-1); last = ((np.append(np.flatnonzero(t)[1:], t.size) - 1) % V)[np.add.accumulate(t) - 1].reshape(N, 8, V)
    if not (np.take_along_axis(e, p, 2) == last).all(): bad.append("en: last places")
    L = np.tile(np.arange(V), (8, 1))
    for i in range(R): L = hop(p, s, L)
    if not (hop(p, s, L) == L).all(): bad.append("at most R steps to the smallest vertex")
    return bad
def reference(pm, en, st):
    p = np.stack([gentries(a) for a in pm]); L = np.tile(np.arange(V), (8, 1))
    while True:
        M = hop(p, st, L)
        if (M == L).all(): break
        L = M
    c = np.count_nonzero(L == np.arange(V), axis=1).reshape(8, 1)
    return {"y": np.stack([L for r in range(N)]).astype(np.float32), "cnt": np.stack([c for r in range(N)]).astype(np.float32)}

@@ -1,0 +1,308 @@
+from concourse.bass import DstId, RemoteDMATransfer
+from concourse.mybir import AluOpType as A, ActivationFunctionType as F
+
+V, R, BLK = 2048, 8, 128
+PR = 64
+CFG = {
+    "pm": [("v", 672), ("s", 928), ("s", 448)],
+    "pieces": [("s", 384, "v"), ("v", 512, "s"), ("s", 288, "s"), ("s", 288, "v"), ("s", 192, "v"), ("v", 384, "v")],
+    "odd": "g0 g1 b0 g5 g3 b1 g4 b3 b4 b5 x0 x3 g2 x4 x1 x5 b2 x2",
+    "chunks": [(2, 4), (4, 2), (1, 3)],
+    "order": "G0 L0 G1 L1 G2 N0 T0 L2 N1 T1 C0 B0 N2 T2 C1 B1 X0.0 X0.1 C2 X1.0 X1.1 B2 X2.0 X2.1",
+    "last": "G0 L0 G1 L1 G2 N0 L2 N1 N2",
+    "copy": "svv",
+    "evac": [[("v", 0, 3), ("s", 3, 3)], [("s", 0, 3), ("v", 3, 3)], [("s", 0, 2), ("v", 2, 2)]],
+}
+NBMAX = 6
+SCALE = 2.0 ** -16
+
+SCRATCH = {
+    "txa": ("dram", [8, 128, 32], "int32"), "rxa": ("dram", [8, 128, 32], "int32"),
+    "txb": ("dram", [8, 128, 16], "int32"), "rxb": ("dram", [8, 128, 16], "int32"),
+    "pmi": ("sbuf", [128, 128], "int32"), "eni": ("sbuf", [128, 128], "int32"),
+    "pmo": ("sbuf", [128, 128], "uint16"), "eno": ("sbuf", [128, 128], "uint16"),
+    "mask": ("sbuf", [128, V], "bfloat16"), "maskall": ("sbuf", [128, V], "bfloat16"),
+    "win": ("sbuf", [128, V], "bfloat16"), "plc": ("sbuf", [128, V], "bfloat16"),
+    "seg": ("sbuf", [128, V], "bfloat16"), "upd": ("sbuf", [128, V], "bfloat16"),
+    "ones": ("sbuf", [128, 128], "bfloat16"), "ident": ("sbuf", [128, 128], "bfloat16"),
+    "identf": ("sbuf", [128, 128], "float32"), "ramp": ("sbuf", [128, 128], "bfloat16"),
+    "sel": ("sbuf", [128, PR], "bfloat16"), "lanes": ("sbuf", [128, 128], "bfloat16"),
+    "spread": ("sbuf", [128, NBMAX * 128], "bfloat16"),
+    "rst": ("sbuf", [128, PR * NBMAX], "bfloat16"), "horn": ("sbuf", [128, 112], "bfloat16"),
+    "low": ("sbuf", [128, 16 * PR], "bfloat16"), "row": ("sbuf", [128, V], "bfloat16"),
+    "clip": ("sbuf", [128, 112], "bfloat16"), "dec": ("sbuf", [128, 112], "float32"),
+    "land": ("sbuf", [128, 128], "float32"), "own": ("sbuf", [128, 128], "float32"),
+    "eq": ("sbuf", [128, 128], "bfloat16"), "lab": ("sbuf", [128, 128], "float32"),
+    "num": ("sbuf", [128, 4], "float32"),
+    "ps_b0": ("psum", [128, 512], "float32"), "ps_b1": ("psum", [128, 512], "float32"),
+    "ps_b2": ("psum", [128, 512], "float32"), "ps_b3": ("psum", [128, 512], "float32"),
+    "ps_s0": ("psum", [128, 512], "float32"), "ps_s1": ("psum", [128, 512], "float32"),
+    "ps_t0": ("psum", [128, 1024], "bfloat16"), "ps_t1": ("psum", [128, 1024], "bfloat16"),
+}
+REMOTE = ["arr_a", "arr_b", "arr_y", "sent"]
+SEMAPHORES = REMOTE + ["q%d" % i for i in range(140)]
+
+
+def emit(queues, ops, sems):
+    batches = {}
+    for i, o in enumerate(ops):
+        batches.setdefault(o["key"], []).append(i)
+    hist, obs, snap, used, waits = {}, {}, {}, {}, []
+    for i, o in enumerate(ops):
+        q, deps = o["q"], []
+        both = [(0, x) for x in o["r"]] + [(1, x) for x in o["w"]]
+        for kind, (b, c0, c1) in both:
+            for (j, d0, d1, w) in hist.get(b, []):
+                cross = b.startswith("ps_") and ops[j]["q"] != q
+                if not cross and (not (kind or w) or d1 <= c0 or c1 <= d0):
+                    continue
+                if ops[j]["key"] != o["key"]:
+                    deps.append(j)
+        for kind, (b, c0, c1) in both:
+            h = hist.setdefault(b, [])
+            if kind and not b.startswith("ps_"):
+                h[:] = [x for x in h if not (c0 <= x[1] and x[2] <= c1) or ops[x[0]]["key"] == o["key"]]
+            elif kind:
+                h[:] = [x for x in h if not (c0 <= x[1] and x[2] <= c1 and ops[x[0]]["q"] == q) or ops[x[0]]["key"] == o["key"]]
+                if len(h) > 120:
+                    h[:] = h[-120:]
+            h.append((i, c0, c1, kind))
+        seen = obs.setdefault(q, {})
+        need = []
+        for j in sorted(set(deps), reverse=True):
+            name, b = ops[j]["key"]
+            if seen.get(name, -1) >= b:
+                continue
+            need.append((name, b))
+            used[name] = True
+            for k in batches[(name, b)]:
+                for n2, b2 in snap[k].items():
+                    if seen.get(n2, -1) < b2:
+                        seen[n2] = b2
+            seen[name] = b
+        waits.append(need)
+        snap[i] = dict(seen)
+    keep = {}
+    for o in ops:
+        n = o["key"][0]
+        if (n in used or o["inc"] == 16) and n not in keep:
+            keep[n] = sems.pop(0)
+    level, total = {}, {}
+    for o in ops:
+        n, b = o["key"]
+        if n in keep:
+            total[n] = total.get(n, 0) + o["inc"]
+            level[(n, b)] = total[n]
+    done = {}
+    for i, o in enumerate(ops):
+        eng = queues[o["q"]]
+        for (s, v) in o["ext"]:
+            eng.wait_ge(s, v)
+        for kb in waits[i]:
+            eng.wait_ge(keep[kb[0]], level[kb])
+            done[kb[0]] = max(done.get(kb[0], 0), level[kb])
+        ins = o["f"]()
+        if o["key"][0] in keep:
+            ins.then_inc(keep[o["key"][0]], o["inc"])
+    for n in keep:
+        if done.get(n, 0) < total[n]:
+            queues["y"].wait_ge(keep[n], total[n])
+
+
+def rank_program(g, core, T, topo):
+    me = T.rank_of(core)
+    if me is None:
+        return
+    cores = list(T.cores)
+    peers = [cores[(me + k) % len(cores)] for k in range(1, len(cores))]
+    queues = {"g": g, "v": g.vector, "s": g.scalar, "t": g.tensor, "y": g.sync}
+    ops = []
+    uniq = [0]
+
+    def op(q, key, f, r=(), w=(), inc=1, ext=()):
+        if key is None:
+            uniq[0] += 1
+            key = ("u%d" % uniq[0], 0)
+        ops.append({"q": q, "key": key, "f": f, "r": list(r), "w": list(w), "inc": inc, "ext": list(ext)})
+
+    def dma(q, key, out, in_, r, w, ext=()):
+        op(q, (key, 0), lambda: queues[q].dma_start(out, in_), r, w, 16, ext)
+
+    def c(n, a=0, b=None):
+        return (n, a, V if b is None else b)
+
+    def dst(d):
+        rid, pid = topo.addr(d)[0:2]
+        return DstId(rid=rid, pnc=pid)
+
+    lo = 16 * me
+    dma("y", "h_pm", T.txa[:, 0:64, :], T.pm[:], [], [c("txa_pm")])
+    dma("s", "h_st", T.txa[:, 64:128, :], T.st[:], [], [c("txa_st")])
+    dma("y", "h_en", T.txb[:], T.en[:], [], [c("txb")])
+    dma("s", "o_pm", T.rxa[me, 0:64, :], T.pm[lo:lo + 16, :], [], [c("rxa_pm")])
+    dma("s", "o_st", T.rxa[me, 64:128, :], T.st[me:me + 1, :], [], [c("rxa_st")])
+    dma("y", "o_en", T.rxb[me], T.en[lo:lo + 16, :], [], [c("rxb")])
+
+    op("v", None, lambda: g.vector.memset(T.ones[:], 1.0), [], [c("ones")])
+    op("g", None, lambda: g.iota(T.ramp[:], [[1, 128]], 0, 0, allow_small_or_imprecise_dtypes=True), [], [c("ramp")])
+    op("g", None, lambda: g.affine_select(T.ident[:], T.ones[:], [[-1, 128]], A.is_equal, 0.0, 0, 1), [c("ones")], [c("ident")])
+    op("g", None, lambda: g.affine_select(T.sel[:], T.ones[:, 0:PR], [[-16, 8], [-1, 8]], A.is_equal, 0.0, 0, 1), [c("ones")], [c("sel")])
+    op("g", None, lambda: g.affine_select(T.lanes[:], T.ones[:], [[0, 8], [0, 2], [-16, 8]], A.is_equal, 0.0, 0, 1), [c("ones")], [c("lanes")])
+
+    es = topo.engines(core, peers[0])[0::2]
+
+    def a2a(tx, rx, arr, r):
+        def f():
+            tr = [RemoteDMATransfer(dst_ids=[dst(d)], dma_engine_mask=1 << es[k], remote_sem=arr,
+                                    srcs=[tx[T.rank_of(d)]], dsts=[rx[me]]) for k, d in enumerate(peers)]
+            return g.remote_dma_fused(tr, local_sem=T.sem.sent)
+        op("g", ("none", 0), f, r, [])
+    a2a(T.txa, T.rxa, T.sem.arr_a, [c("txa_pm"), c("txa_st")])
+    a2a(T.txb, T.rxb, T.sem.arr_b, [c("txb")])
+    n_in = len(peers)
+
+    op("v", None, lambda: g.vector.memset(T.mask[:], 0.0), [], [c("mask")])
+
+    def ramp(e):
+        m = 2.0 ** max((e - 8 if e >= 8 else 7 - e) - 1, 0)
+        a = 0.0 if e == 8 else (-128.0 if e == 7 else (128.0 if e > 7 else -256.0))
+        return lambda: g.vector.tensor_scalar(T.win[:, 128 * e:128 * e + 128], T.ramp[:], m * SCALE, a * m * SCALE, A.mult, A.add)
+    for e in range(16):
+        op("v", ("w0", 0), ramp(e), [c("ramp")], [c("win", 128 * e, 128 * e + 128)])
+    op("v", ("k_a", 0), lambda: g.vector.memset(T.rst[:], 0.0), [], [c("rst")])
+    op("v", ("k_b", 0), lambda: g.vector.memset(T.rst[:, 0::PR], 1.0), [], [c("rst")])
+
+    def spread(b):
+        return lambda: g.vector.tensor_scalar(T.spread[:, 128 * b:128 * b + 128], T.ones[:], T.ident[:, b:b + 1], None, A.mult)
+    for b in range(NBMAX):
+        op("v", ("spr", 0), spread(b), [c("ones"), c("ident")], [c("spread", 128 * b, 128 * b + 128)])
+    op("v", ("k_c", 0), lambda: g.vector.memset(T.horn[:], 2.0), [], [c("horn")])
+    op("v", ("k_d", 0), lambda: g.vector.memset(T.horn[:, 0::7], 0.0), [], [c("horn")])
+    op("v", ("k_e", 0), lambda: g.vector.memset(T.horn[:, 6::7], 1.0), [], [c("horn")])
+    op("v", ("k_f", 0), lambda: g.vector.tensor_copy(T.identf[:], T.ident[:]), [c("ident")], [c("identf")])
+    op("v", None, lambda: g.vector.memset(T.maskall[:], 0.0), [], [c("maskall")])
+
+    dma("y", "l_pm", T.pmi[:], T.rxa[:, 0:64, :], [c("rxa_pm")], [c("pmi")], [(T.sem.arr_a, n_in)])
+    dma("g", "l_st", T.mask[0:128:16, :], T.rxa[:, 64:128, :], [c("rxa_st")], [c("mask")], [(T.sem.arr_a, n_in)])
+    dma("y", "l_en", T.eni[:], T.rxb[:], [c("rxb")], [c("eni")], [(T.sem.arr_b, n_in)])
+    for i in range(8):
+        dma("y", "m_%d" % i, T.maskall[i:128:16, :], T.mask[0:128:16, :], [c("mask")], [("maskall", i, i + 1)])
+    op("g", None, lambda: g.iota(T.own[:], [[0, 8], [128, 16]], 0, 1, allow_small_or_imprecise_dtypes=True), [], [c("own")])
+    op("v", None, lambda: g.vector.tensor_copy(T.pmo[:], T.pmi[:]), [c("pmi")], [c("pmo")])
+
+    starts, b0 = [], 0
+    for nv, ns in CFG["chunks"]:
+        starts.append(b0)
+        b0 += nv + ns
+    bank, banks = [0], {}
+
+    def copy(q, key, o, i, r, w):
+        f = (lambda: g.vector.tensor_copy(o, i)) if q == "v" else (lambda: g.scalar.activation(o, i, F.Copy))
+        op(q, key, f, r, w)
+
+    def gather(q, key, out, win, off, a, b):
+        copy(q, key, T[out][:, a:b], T[win][:, 0:V].indirect(T[off][:, a // 16:b // 16]), [c(win), c(off)], [c(out, a, b)])
+
+    def places(r):
+        a = 0
+        for k, (q, n) in enumerate(CFG["pm"]):
+            gather(q, ("p%d" % k, r), "plc", "win", "pmo", a, a + n)
+            a += n
+        a, m = 0, "mask" if r == 0 else "maskall"
+        for k, (q, n) in enumerate(CFG["pm"]):
+            def f(a=a, n=n):
+                init = 0.0 if a == 0 else T.seg[:, a - 1:a]
+                return g.vector.tensor_tensor_scan(T.seg[:, a:a + n], T[m][:, a:a + n], T.plc[:, a:a + n], init, A.add, A.min)
+            op("v", ("c%d" % k, r), f, [c(m), c("plc", a, a + n)] + ([c("seg", a - 1, a)] if a else []), [c("seg", a, a + n)])
+            a += n
+
+    def merge_stage(t, i, r, piece):
+        nv, ns = CFG["chunks"][i]
+        s, nb = starts[i], nv + ns
+        p, pt = "ps_s%d" % (i % 2), "ps_t%d" % (i % 2)
+        row, low = c("row", BLK * i, BLK * i + BLK), c("low", PR * s, PR * (s + nb))
+        if t == "G":
+            gather("v", ("gv%d" % i, r), "upd", "seg", "eno", BLK * s, BLK * (s + nv))
+            gather("s", ("gs%d" % i, r), "upd", "seg", "eno", BLK * (s + nv), BLK * (s + nb))
+        elif t == "L":
+            for b in range(nb):
+                v0 = BLK * (s + b)
+                op("t", ("l%d" % i, r), lambda b=b, v0=v0: g.tensor.matmul(T[p][:, PR * b:PR * b + PR], T.upd[:, v0:v0 + BLK], T.sel[:], True, True),
+                   [c("upd", v0, v0 + BLK), c("sel")], [c(p, PR * b, PR * b + PR)])
+        elif t == "N":
+            op("v", ("n%d" % i, r), lambda: g.vector.tensor_tensor_scan(T.low[:, PR * s:PR * (s + nb)], T.rst[:, 0:PR * nb], T[p][:, 0:PR * nb], 0.0, A.add, A.min),
+               [c("rst"), c(p, 0, PR * nb)], [low])
+        elif t == "T":
+            op("t", ("t%d" % i, r), lambda: g.tensor.transpose(T[pt][0:nb, 0:BLK], T.low[:, PR * s + PR - 1:PR * (s + nb):PR], T.ident[:]),
+               [low, c("ident")], [c(pt, 0, BLK)])
+        elif t == "C":
+            copy(CFG["copy"][i], ("y%d" % i, r), T.row[0:nb, BLK * i:BLK * i + BLK], T[pt][0:nb, 0:BLK], [c(pt, 0, BLK)], [row])
+        elif t == "B":
+            for k, (q, e0, n) in enumerate(CFG["evac"][i]):
+                pb = banks[(i, k)] = "ps_b%d" % (bank[0] % 4)
+                bank[0] += 1
+                for b in range(n):
+                    op("t", ("b%d_%d" % (i, k), r),
+                       lambda b=b, e=e0 + b, pb=pb: g.tensor.matmul(T[pb][:, BLK * b:BLK * b + BLK], T.spread[0:nb, BLK * e:BLK * e + BLK],
+                                                                    T.row[0:nb, BLK * i:BLK * i + BLK], True, True),
+                       [c("spread"), row], [c(pb, BLK * b, BLK * b + BLK)])
+        elif t == "X":
+            q, e0, n = CFG["evac"][i][piece]
+            pb, v0 = banks[(i, piece)], BLK * (s + e0)
+            copy(q, ("x%d_%d" % (i, piece), r), T.win[:, v0:v0 + BLK * n], T[pb][:, 0:BLK * n], [c(pb, 0, BLK * n)], [c("win", v0, v0 + BLK * n)])
+
+    pieces, a = [], 0
+    for (q, n, x) in CFG["pieces"]:
+        pieces.append((q, a, a + n, x, ("ps_b0", "ps_b1", "ps_b2", "ps_b3", "ps_s0", "ps_s1")[len(pieces)]))
+        a += n
+
+    def spread_stage(t, k, r):
+        q, a, b, x, pb = pieces[k]
+        if t == "g":
+            gather(q, ("og%d" % k, r), "upd", "seg", "eno", a, b)
+        elif t == "b":
+            op("t", ("ob%d" % k, r), lambda: g.tensor.matmul(T[pb][:, 0:b - a], T.lanes[:], T.upd[:, a:b], True, True),
+               [c("lanes"), c("upd", a, b)], [c(pb, 0, b - a)])
+        else:
+            copy(x, ("ox%d" % k, r), T.win[:, a:b], T[pb][:, 0:b - a], [c(pb, 0, b - a)], [c("win", a, b)])
+
+    for r in range(R):
+        places(r)
+        if r == 0:
+            op("v", None, lambda: g.vector.tensor_copy(T.eno[:], T.eni[:]), [c("eni")], [c("eno")])
+        if r % 2 == 0:
+            for tok in CFG["odd"].split():
+                spread_stage(tok[0], int(tok[1:]), r)
+        else:
+            for tok in (CFG["order"] if r < R - 1 else CFG["last"]).split():
+                tk = tok[1:].split(".")
+                merge_stage(tok[0], int(tk[0]), r, int(tk[1]) if len(tk) > 1 else None)
+
+    for k in range(7):
+        if k < 6:
+            lim = 256.0 * 2.0 ** k * SCALE
+            f = lambda k=k, lim=lim: g.vector.tensor_scalar(T.clip[:, k::7], T.low[:, PR - 1::PR], lim, -lim, A.min, A.max)
+        else:
+            f = lambda: g.vector.tensor_copy(T.clip[:, 6::7], T.low[:, PR - 1::PR])
+        op("v", ("clip", 0), f, [c("low")], [c("clip")])
+    op("v", ("dec", 0), lambda: g.vector.tensor_tensor_scan(T.dec[:], T.horn[:], T.clip[:], 0.0, A.mult, A.add), [c("horn"), c("clip")], [c("dec")])
+    l0 = 16 * me
+    mine = T.land[:, l0:l0 + 16]
+    op("v", ("lab", 0), lambda: g.vector.tensor_scalar(mine, T.dec[:, 6::7], 2.0 ** -6 / SCALE, 1024.0, A.mult, A.add), [c("dec")], [c("land", l0, l0 + 16)])
+
+    def bcast():
+        return g.remote_dma_fused([RemoteDMATransfer(dst_ids=[dst(d) for d in peers], dma_engine_mask=sum(1 << e for e in es), remote_sem=T.sem.arr_y,
+                                                     srcs=[mine], dsts=[mine for d in peers])], local_sem=T.sem.sent)
+    op("g", ("none", 1), bcast, [c("land", l0, l0 + 16)], [])
+    arr = [(T.sem.arr_y, len(es) * len(peers))]
+    op("t", ("fin_t", 0), lambda: g.tensor.transpose(T.ps_b0[:, 0:128], T.land[:], T.identf[:]), [c("land", l0, l0 + 16), c("identf")], [c("ps_b0", 0, 128)], 1, arr)
+    op("v", ("fin_e", 0), lambda: g.vector.tensor_tensor(T.eq[:], T.land[:], T.own[:], A.is_equal), [c("land", l0, l0 + 16), c("own")], [c("eq")], 1, arr)
+    copy("s", ("fin_l", 0), T.lab[:], T.ps_b0[:, 0:128], [c("ps_b0", 0, 128)], [c("lab")])
+    for b in range(16):
+        op("t", ("fin_n", 0), lambda b=b: g.tensor.matmul(T.ps_s0[0:8, 0:1], T.eq[:, b::16], T.ones[:, 0:1], b == 0, b == 15), [c("eq"), c("ones")], [c("ps_s0", 0, 1)])
+    copy("v", ("fin_c", 0), T.num[0:8, 0:1], T.ps_s0[0:8, 0:1], [c("ps_s0", 0, 1)], [c("num")])
+    dma("s", "st_y", T.y[:], T.lab[:], [c("lab")], [])
+    dma("y", "st_c", T.cnt[:], T.num[0:8, 0:1], [c("num")], [])
+
+    emit(queues, ops, [T.sem["q%d" % i] for i in range(140)])
+    g.wait_ge(T.sem.sent, 2 * n_in + len(es))

@@ -2,44 +2,53 @@ from concourse.bass import DstId, RemoteDMATransfer
 from concourse.mybir import AluOpType as A, ActivationFunctionType as F
 
 V, R, BLK = 2048, 8, 128
-PR = 64
+NB = V // BLK
+ONE, TWO = 16, 64
 CFG = {
-    "pm": [("v", 672), ("s", 928), ("s", 448)],
-    "pieces": [("s", 384, "v"), ("v", 512, "s"), ("s", 288, "s"), ("s", 288, "v"), ("s", 192, "v"), ("v", 384, "v")],
-    "odd": "g0 g1 b0 g5 g3 b1 g4 b3 b4 b5 x0 x3 g2 x4 x1 x5 b2 x2",
-    "chunks": [(2, 4), (4, 2), (1, 3)],
-    "order": "G0 L0 G1 L1 G2 N0 T0 L2 N1 T1 C0 B0 N2 T2 C1 B1 X0.0 X0.1 C2 X1.0 X1.1 B2 X2.0 X2.1",
-    "last": "G0 L0 G1 L1 G2 N0 L2 N1 N2",
-    "copy": "svv",
-    "evac": [[("v", 0, 3), ("s", 3, 3)], [("s", 0, 3), ("v", 3, 3)], [("s", 0, 2), ("v", 2, 2)]],
+    "pm": ([("v", 640), ("s", 640), ("s", 608), ("v", 160)], [1280, 768]),
+    "pm0": ([("v", 704), ("s", 320), ("s", 928), ("v", 96)], [1024, 1024]),
+    "spread": {"u": 32, "g": [("v", 14), ("s", 21), ("v", 15), ("s", 14)], "n": [],
+               "x": [("v", 11), ("s", 8), ("v", 16), ("s", 15), ("v", 10), ("s", 4)],
+               "order": "G0 G1 G2 G3 B0 X0 B1 X1 B2 X2 B3 X3 B4 X4 B5 X5"},
+    "merge": {"u": BLK, "g": [("v", 3), ("s", 5), ("v", 4), ("s", 4)], "n": [1, 1, 1, 1],
+              "x": [("s", 2), ("v", 6), ("s", 4), ("v", 4)],
+              "order": "G0 G1 G2 G3 L0 L1 N0 L2 T0 N1 L3 N2 X0 N3 T1 T2 X1 T3 X2 X3"},
+    "last": {"u": BLK, "g": [("v", 5), ("s", 6), ("v", 2), ("s", 2), ("v", 1)], "n": [1, 2, 2], "x": [],
+             "order": "G0 G1 G2 G3 G4 L0 L1 L2 N0 L3 L4 N1 N2"},
+    "own": [("v", 6), ("s", 6), ("v", 2), ("s", 2)],
+    "x0": [("v", 6), ("s", 4), ("v", 3), ("v", 3)],
+    "codes_late": 2, "stt": "v",
+    "codes_s": 7,
+    "engines": 2,
 }
-NBMAX = 6
 SCALE = 2.0 ** -16
 
 SCRATCH = {
     "txa": ("dram", [8, 128, 32], "int32"), "rxa": ("dram", [8, 128, 32], "int32"),
-    "txb": ("dram", [8, 128, 16], "int32"), "rxb": ("dram", [8, 128, 16], "int32"),
+    "txs": ("dram", [8, 128, 16], "bfloat16"), "rxs": ("dram", [8, 128, 16], "bfloat16"),
+    "sti": ("sbuf", [128, 128], "int32"), "stb": ("sbuf", [128, 128], "bfloat16"), "stt": ("sbuf", [128, 144], "bfloat16"),
+    "pmi0": ("sbuf", [128, 128], "int32"), "eni0": ("sbuf", [128, 128], "int32"),
+    "pmo0": ("sbuf", [128, 128], "uint16"), "eno0": ("sbuf", [128, 128], "uint16"),
     "pmi": ("sbuf", [128, 128], "int32"), "eni": ("sbuf", [128, 128], "int32"),
     "pmo": ("sbuf", [128, 128], "uint16"), "eno": ("sbuf", [128, 128], "uint16"),
-    "mask": ("sbuf", [128, V], "bfloat16"), "maskall": ("sbuf", [128, V], "bfloat16"),
-    "win": ("sbuf", [128, V], "bfloat16"), "plc": ("sbuf", [128, V], "bfloat16"),
-    "seg": ("sbuf", [128, V], "bfloat16"), "upd": ("sbuf", [128, V], "bfloat16"),
-    "ones": ("sbuf", [128, 128], "bfloat16"), "ident": ("sbuf", [128, 128], "bfloat16"),
-    "identf": ("sbuf", [128, 128], "float32"), "ramp": ("sbuf", [128, 128], "bfloat16"),
-    "sel": ("sbuf", [128, PR], "bfloat16"), "lanes": ("sbuf", [128, 128], "bfloat16"),
-    "spread": ("sbuf", [128, NBMAX * 128], "bfloat16"),
-    "rst": ("sbuf", [128, PR * NBMAX], "bfloat16"), "horn": ("sbuf", [128, 112], "bfloat16"),
-    "low": ("sbuf", [128, 16 * PR], "bfloat16"), "row": ("sbuf", [128, V], "bfloat16"),
-    "clip": ("sbuf", [128, 112], "bfloat16"), "dec": ("sbuf", [128, 112], "float32"),
-    "land": ("sbuf", [128, 128], "float32"), "own": ("sbuf", [128, 128], "float32"),
-    "eq": ("sbuf", [128, 128], "bfloat16"), "lab": ("sbuf", [128, 128], "float32"),
-    "num": ("sbuf", [128, 4], "float32"),
-    "ps_b0": ("psum", [128, 512], "float32"), "ps_b1": ("psum", [128, 512], "float32"),
-    "ps_b2": ("psum", [128, 512], "float32"), "ps_b3": ("psum", [128, 512], "float32"),
-    "ps_s0": ("psum", [128, 512], "float32"), "ps_s1": ("psum", [128, 512], "float32"),
+    "roi": ("sbuf", [128, 16], "int32"), "roj": ("sbuf", [128, 16], "int32"), "roo": ("sbuf", [128, 16], "uint16"),
+    "win": ("sbuf", [128, V], "bfloat16"), "mask": ("sbuf", [128, V], "bfloat16"),
+    "plc": ("sbuf", [128, V], "bfloat16"), "seg": ("sbuf", [128, V], "bfloat16"), "upd": ("sbuf", [128, V], "bfloat16"),
+    "z16": ("sbuf", [128, 16 * ONE * NB], "bfloat16"), "z64": ("sbuf", [128, 16 * TWO * NB], "bfloat16"),
+    "ones": ("sbuf", [128, 128], "bfloat16"), "ident": ("sbuf", [128, 128], "bfloat16"), "ramp": ("sbuf", [128, 128], "bfloat16"),
+    "lanes": ("sbuf", [128, 128], "bfloat16"),
+    "sel16": ("sbuf", [128, ONE], "bfloat16"), "rst16": ("sbuf", [128, ONE * NB], "bfloat16"),
+    "sel64": ("sbuf", [128, TWO], "bfloat16"), "rst64": ("sbuf", [128, TWO * 8], "bfloat16"),
+    "tx1": ("sbuf", [128, 128], "bfloat16"), "land1": ("sbuf", [128, 128], "bfloat16"), "ro": ("sbuf", [128, ONE * NB], "bfloat16"),
+    "ownc": ("sbuf", [128, NB], "bfloat16"), "land2": ("sbuf", [128, 256], "bfloat16"),
+    "wid": ("sbuf", [128, 6 * 128], "bfloat16"), "clip": ("sbuf", [128, 6 * 128], "bfloat16"),
+    "lab": ("sbuf", [128, 128], "float32"), "num": ("sbuf", [128, 4], "float32"),
+    "ps_l0": ("psum", [128, 512], "float32"), "ps_l1": ("psum", [128, 512], "float32"),
+    "ps_l2": ("psum", [128, 512], "float32"), "ps_l3": ("psum", [128, 512], "float32"),
     "ps_t0": ("psum", [128, 1024], "bfloat16"), "ps_t1": ("psum", [128, 1024], "bfloat16"),
+    "ps_t2": ("psum", [128, 1024], "bfloat16"), "ps_t3": ("psum", [128, 1024], "bfloat16"),
 }
-REMOTE = ["arr_a", "arr_b", "arr_y", "sent"]
+REMOTE = ["arr_a", "arr_b", "arr_c", "arr_y", "sent"]
 SEMAPHORES = REMOTE + ["q%d" % i for i in range(140)]
 
 
@@ -109,12 +118,21 @@ def emit(queues, ops, sems):
             queues["y"].wait_ge(keep[n], total[n])
 
 
+def runs(pieces, unit=1):
+    out, a = [], 0
+    for q, n in pieces:
+        out.append((q, a, a + n * unit))
+        a += n * unit
+    return out
+
+
 def rank_program(g, core, T, topo):
     me = T.rank_of(core)
     if me is None:
         return
     cores = list(T.cores)
     peers = [cores[(me + k) % len(cores)] for k in range(1, len(cores))]
+    n_in = len(peers)
     queues = {"g": g, "v": g.vector, "s": g.scalar, "t": g.tensor, "y": g.sync}
     ops = []
     uniq = [0]
@@ -129,180 +147,216 @@ def rank_program(g, core, T, topo):
         op(q, (key, 0), lambda: queues[q].dma_start(out, in_), r, w, 16, ext)
 
     def c(n, a=0, b=None):
-        return (n, a, V if b is None else b)
+        return (n, a, 8 * V if b is None else b)
 
     def dst(d):
         rid, pid = topo.addr(d)[0:2]
         return DstId(rid=rid, pnc=pid)
 
-    lo = 16 * me
-    dma("y", "h_pm", T.txa[:, 0:64, :], T.pm[:], [], [c("txa_pm")])
-    dma("s", "h_st", T.txa[:, 64:128, :], T.st[:], [], [c("txa_st")])
-    dma("y", "h_en", T.txb[:], T.en[:], [], [c("txb")])
-    dma("s", "o_pm", T.rxa[me, 0:64, :], T.pm[lo:lo + 16, :], [], [c("rxa_pm")])
-    dma("s", "o_st", T.rxa[me, 64:128, :], T.st[me:me + 1, :], [], [c("rxa_st")])
-    dma("y", "o_en", T.rxb[me], T.en[lo:lo + 16, :], [], [c("rxb")])
-
-    op("v", None, lambda: g.vector.memset(T.ones[:], 1.0), [], [c("ones")])
-    op("g", None, lambda: g.iota(T.ramp[:], [[1, 128]], 0, 0, allow_small_or_imprecise_dtypes=True), [], [c("ramp")])
-    op("g", None, lambda: g.affine_select(T.ident[:], T.ones[:], [[-1, 128]], A.is_equal, 0.0, 0, 1), [c("ones")], [c("ident")])
-    op("g", None, lambda: g.affine_select(T.sel[:], T.ones[:, 0:PR], [[-16, 8], [-1, 8]], A.is_equal, 0.0, 0, 1), [c("ones")], [c("sel")])
-    op("g", None, lambda: g.affine_select(T.lanes[:], T.ones[:], [[0, 8], [0, 2], [-16, 8]], A.is_equal, 0.0, 0, 1), [c("ones")], [c("lanes")])
-
-    es = topo.engines(core, peers[0])[0::2]
-
-    def a2a(tx, rx, arr, r):
-        def f():
-            tr = [RemoteDMATransfer(dst_ids=[dst(d)], dma_engine_mask=1 << es[k], remote_sem=arr,
-                                    srcs=[tx[T.rank_of(d)]], dsts=[rx[me]]) for k, d in enumerate(peers)]
-            return g.remote_dma_fused(tr, local_sem=T.sem.sent)
-        op("g", ("none", 0), f, r, [])
-    a2a(T.txa, T.rxa, T.sem.arr_a, [c("txa_pm"), c("txa_st")])
-    a2a(T.txb, T.rxb, T.sem.arr_b, [c("txb")])
-    n_in = len(peers)
-
-    op("v", None, lambda: g.vector.memset(T.mask[:], 0.0), [], [c("mask")])
-
-    def ramp(e):
-        m = 2.0 ** max((e - 8 if e >= 8 else 7 - e) - 1, 0)
-        a = 0.0 if e == 8 else (-128.0 if e == 7 else (128.0 if e > 7 else -256.0))
-        return lambda: g.vector.tensor_scalar(T.win[:, 128 * e:128 * e + 128], T.ramp[:], m * SCALE, a * m * SCALE, A.mult, A.add)
-    for e in range(16):
-        op("v", ("w0", 0), ramp(e), [c("ramp")], [c("win", 128 * e, 128 * e + 128)])
-    op("v", ("k_a", 0), lambda: g.vector.memset(T.rst[:], 0.0), [], [c("rst")])
-    op("v", ("k_b", 0), lambda: g.vector.memset(T.rst[:, 0::PR], 1.0), [], [c("rst")])
-
-    def spread(b):
-        return lambda: g.vector.tensor_scalar(T.spread[:, 128 * b:128 * b + 128], T.ones[:], T.ident[:, b:b + 1], None, A.mult)
-    for b in range(NBMAX):
-        op("v", ("spr", 0), spread(b), [c("ones"), c("ident")], [c("spread", 128 * b, 128 * b + 128)])
-    op("v", ("k_c", 0), lambda: g.vector.memset(T.horn[:], 2.0), [], [c("horn")])
-    op("v", ("k_d", 0), lambda: g.vector.memset(T.horn[:, 0::7], 0.0), [], [c("horn")])
-    op("v", ("k_e", 0), lambda: g.vector.memset(T.horn[:, 6::7], 1.0), [], [c("horn")])
-    op("v", ("k_f", 0), lambda: g.vector.tensor_copy(T.identf[:], T.ident[:]), [c("ident")], [c("identf")])
-    op("v", None, lambda: g.vector.memset(T.maskall[:], 0.0), [], [c("maskall")])
-
-    dma("y", "l_pm", T.pmi[:], T.rxa[:, 0:64, :], [c("rxa_pm")], [c("pmi")], [(T.sem.arr_a, n_in)])
-    dma("g", "l_st", T.mask[0:128:16, :], T.rxa[:, 64:128, :], [c("rxa_st")], [c("mask")], [(T.sem.arr_a, n_in)])
-    dma("y", "l_en", T.eni[:], T.rxb[:], [c("rxb")], [c("eni")], [(T.sem.arr_b, n_in)])
-    for i in range(8):
-        dma("y", "m_%d" % i, T.maskall[i:128:16, :], T.mask[0:128:16, :], [c("mask")], [("maskall", i, i + 1)])
-    op("g", None, lambda: g.iota(T.own[:], [[0, 8], [128, 16]], 0, 1, allow_small_or_imprecise_dtypes=True), [], [c("own")])
-    op("v", None, lambda: g.vector.tensor_copy(T.pmo[:], T.pmi[:]), [c("pmi")], [c("pmo")])
-
-    starts, b0 = [], 0
-    for nv, ns in CFG["chunks"]:
-        starts.append(b0)
-        b0 += nv + ns
-    bank, banks = [0], {}
-
-    def copy(q, key, o, i, r, w):
+    def copy(q, key, o, i, r, w, ext=()):
         f = (lambda: g.vector.tensor_copy(o, i)) if q == "v" else (lambda: g.scalar.activation(o, i, F.Copy))
-        op(q, key, f, r, w)
+        op(q, key, f, r, w, 1, ext)
 
-    def gather(q, key, out, win, off, a, b):
-        copy(q, key, T[out][:, a:b], T[win][:, 0:V].indirect(T[off][:, a // 16:b // 16]), [c(win), c(off)], [c(out, a, b)])
+    def gather(q, key, out, win, off, a, b, ext=()):
+        copy(q, key, T[out[0]][:, out[1] + a:out[1] + b], T[win[0]][:, win[1]:win[1] + win[2]].indirect(T[off][:, a // 16:b // 16]),
+             [c(win[0], win[1], win[1] + win[2]), c(off)], [c(out[0], out[1] + a, out[1] + b)], ext)
 
-    def places(r):
-        a = 0
-        for k, (q, n) in enumerate(CFG["pm"]):
-            gather(q, ("p%d" % k, r), "plc", "win", "pmo", a, a + n)
-            a += n
-        a, m = 0, "mask" if r == 0 else "maskall"
-        for k, (q, n) in enumerate(CFG["pm"]):
-            def f(a=a, n=n):
-                init = 0.0 if a == 0 else T.seg[:, a - 1:a]
-                return g.vector.tensor_tensor_scan(T.seg[:, a:a + n], T[m][:, a:a + n], T.plc[:, a:a + n], init, A.add, A.min)
-            op("v", ("c%d" % k, r), f, [c(m), c("plc", a, a + n)] + ([c("seg", a - 1, a)] if a else []), [c("seg", a, a + n)])
-            a += n
+    def matmul(key, out, lhs, rhs, r, w, start=True, stop=True, ext=()):
+        op("t", key, lambda: g.tensor.matmul(out, lhs, rhs, start, stop), r, w, 1, ext)
 
-    def merge_stage(t, i, r, piece):
-        nv, ns = CFG["chunks"][i]
-        s, nb = starts[i], nv + ns
-        p, pt = "ps_s%d" % (i % 2), "ps_t%d" % (i % 2)
-        row, low = c("row", BLK * i, BLK * i + BLK), c("low", PR * s, PR * (s + nb))
-        if t == "G":
-            gather("v", ("gv%d" % i, r), "upd", "seg", "eno", BLK * s, BLK * (s + nv))
-            gather("s", ("gs%d" % i, r), "upd", "seg", "eno", BLK * (s + nv), BLK * (s + nb))
-        elif t == "L":
-            for b in range(nb):
-                v0 = BLK * (s + b)
-                op("t", ("l%d" % i, r), lambda b=b, v0=v0: g.tensor.matmul(T[p][:, PR * b:PR * b + PR], T.upd[:, v0:v0 + BLK], T.sel[:], True, True),
-                   [c("upd", v0, v0 + BLK), c("sel")], [c(p, PR * b, PR * b + PR)])
-        elif t == "N":
-            op("v", ("n%d" % i, r), lambda: g.vector.tensor_tensor_scan(T.low[:, PR * s:PR * (s + nb)], T.rst[:, 0:PR * nb], T[p][:, 0:PR * nb], 0.0, A.add, A.min),
-               [c("rst"), c(p, 0, PR * nb)], [low])
-        elif t == "T":
-            op("t", ("t%d" % i, r), lambda: g.tensor.transpose(T[pt][0:nb, 0:BLK], T.low[:, PR * s + PR - 1:PR * (s + nb):PR], T.ident[:]),
-               [low, c("ident")], [c(pt, 0, BLK)])
-        elif t == "C":
-            copy(CFG["copy"][i], ("y%d" % i, r), T.row[0:nb, BLK * i:BLK * i + BLK], T[pt][0:nb, 0:BLK], [c(pt, 0, BLK)], [row])
-        elif t == "B":
-            for k, (q, e0, n) in enumerate(CFG["evac"][i]):
-                pb = banks[(i, k)] = "ps_b%d" % (bank[0] % 4)
-                bank[0] += 1
-                for b in range(n):
-                    op("t", ("b%d_%d" % (i, k), r),
-                       lambda b=b, e=e0 + b, pb=pb: g.tensor.matmul(T[pb][:, BLK * b:BLK * b + BLK], T.spread[0:nb, BLK * e:BLK * e + BLK],
-                                                                    T.row[0:nb, BLK * i:BLK * i + BLK], True, True),
-                       [c("spread"), row], [c(pb, BLK * b, BLK * b + BLK)])
-        elif t == "X":
-            q, e0, n = CFG["evac"][i][piece]
-            pb, v0 = banks[(i, piece)], BLK * (s + e0)
-            copy(q, ("x%d_%d" % (i, piece), r), T.win[:, v0:v0 + BLK * n], T[pb][:, 0:BLK * n], [c(pb, 0, BLK * n)], [c("win", v0, v0 + BLK * n)])
+    def transpose(key, bank, o, in_, r):
+        op("t", key, lambda: g.tensor.transpose(T[bank][:, o:o + BLK], in_, T.ident[:]), [r, c("ident")], [c(bank, o, o + BLK)])
 
-    pieces, a = [], 0
-    for (q, n, x) in CFG["pieces"]:
-        pieces.append((q, a, a + n, x, ("ps_b0", "ps_b1", "ps_b2", "ps_b3", "ps_s0", "ps_s1")[len(pieces)]))
-        a += n
+    def select(name, pattern, base):
+        n = T[name].shape[1]
+        op("g", None, lambda: g.affine_select(T[name][:], T.ones[:, 0:n], pattern, A.is_equal, 0.0, base, 1), [c("ones")], [c(name)])
 
-    def spread_stage(t, k, r):
-        q, a, b, x, pb = pieces[k]
-        if t == "g":
-            gather(q, ("og%d" % k, r), "upd", "seg", "eno", a, b)
-        elif t == "b":
-            op("t", ("ob%d" % k, r), lambda: g.tensor.matmul(T[pb][:, 0:b - a], T.lanes[:], T.upd[:, a:b], True, True),
-               [c("lanes"), c("upd", a, b)], [c(pb, 0, b - a)])
+    def memset(ap, value, w):
+        op("v", None, lambda: g.vector.memset(ap, value), [], [w])
+
+    es, ne = topo.engines(core, peers[0]), CFG["engines"]
+    eng = [es[ne * k:ne * k + ne] for k in range(n_in)]
+    n_all = ne * (n_in + 1)
+
+    def a2a(n, src, to, arr, r):
+        def f():
+            tr = [RemoteDMATransfer(dst_ids=[dst(d)], dma_engine_mask=sum(1 << e for e in eng[k]), remote_sem=arr,
+                                    srcs=[src(T.rank_of(d))], dsts=[to]) for k, d in enumerate(peers)]
+            return g.remote_dma_fused(tr, local_sem=T.sem.sent)
+        op("g", ("none", n), f, r, [])
+
+    lo = 16 * me
+    dma("s", "n_st", T.sti[:], T.st[:], [], [c("sti")])
+    dma("y", "n_pm", T.pmi0[:], T.pm[:], [], [c("pmi0")])
+    dma("y", "h_pm", T.txa[:, 0:64, :], T.pm[:], [], [c("txa_pm")])
+    dma("y", "h_en", T.txa[:, 64:128, :], T.en[:], [], [c("txa_en")])
+    dma("y", "n_en", T.eni0[:], T.en[:], [], [c("eni0")])
+    dma("y", "o_pm", T.rxa[me, 0:64, :], T.pm[lo:lo + 16, :], [], [c("rxa_pm")])
+    dma("y", "o_en", T.rxa[me, 64:128, :], T.en[lo:lo + 16, :], [], [c("rxa_en")])
+    memset(T.ones[:], 1.0, c("ones"))
+    memset(T.stt[:, 128:144], 0.0, c("stt", 128, 144))
+    memset(T.rst16[:], 0.0, c("rst16"))
+    op("g", None, lambda: g.iota(T.ramp[:], [[1, 128]], 0, 0, allow_small_or_imprecise_dtypes=True), [], [c("ramp")])
+    select("ident", [[-1, 128]], 0)
+    select("sel16", [[0, 2], [-16, 8]], 0)
+    op("g", None, lambda: g.iota(T.roi[:], [[1, NB]], 0, NB), [], [c("roi")])
+    a2a(0, lambda q: T.txa[q], T.rxa[me], T.sem.arr_a, [c("txa_pm"), c("txa_en")])
+
+    def codes(q, e):
+        m = 2.0 ** max((e - 8 if e >= 8 else 7 - e) - 1, 0) * SCALE
+        a = 0.0 if e == 8 else (-128.0 if e == 7 else (128.0 if e > 7 else -256.0))
+        o = T.win[:, BLK * e:BLK * e + BLK]
+        if q == "v":
+            f = lambda: g.vector.tensor_scalar(o, T.ramp[:], m, a * m, A.mult, A.add)
         else:
-            copy(x, ("ox%d" % k, r), T.win[:, a:b], T[pb][:, 0:b - a], [c(pb, 0, b - a)], [c("win", a, b)])
+            f = lambda: g.scalar.activation(o, T.ramp[:], F.Copy, bias=a * m, scale=m)
+        op(q, ("w0" + q, 0), f, [c("ramp")], [c("win", BLK * e, BLK * e + BLK)])
+    late = NB - CFG["codes_late"]
+    for e in range(late):
+        codes("s" if e < CFG["codes_s"] else "v", e)
 
-    for r in range(R):
-        places(r)
-        if r == 0:
-            op("v", None, lambda: g.vector.tensor_copy(T.eno[:], T.eni[:]), [c("eni")], [c("eno")])
-        if r % 2 == 0:
-            for tok in CFG["odd"].split():
-                spread_stage(tok[0], int(tok[1:]), r)
-        else:
-            for tok in (CFG["order"] if r < R - 1 else CFG["last"]).split():
-                tk = tok[1:].split(".")
-                merge_stage(tok[0], int(tk[0]), r, int(tk[1]) if len(tk) > 1 else None)
+    copy("v", None, T.stb[:], T.sti[:], [c("sti")], [c("stb")])
+    copy("v", None, T.pmo0[:], T.pmi0[:], [c("pmi0")], [c("pmo0")])
+    for e in range(late, NB):
+        codes("v", e)
+    transpose(None, "ps_t2", 0, T.stb[:], c("stb"))
+    copy(CFG["stt"], None, T.stt[:, 0:BLK], T.ps_t2[:, 0:BLK], [c("ps_t2", 0, BLK)], [c("stt", 0, BLK)])
+    for b in range(NB):
+        transpose(("fl%d" % (b // 8), 0), "ps_t%d" % (b // 8), BLK * (b % 8), T.stt[:, b:b + BLK], c("stt"))
+    dma("y", "h_st", T.txs[:], T.stb[:], [c("stb")], [c("txs")])
+    dma("y", "o_st", T.rxs[me], T.stb[lo:lo + 16, :], [c("stb")], [c("rxs")])
+    dma("y", "l_pm", T.pmi[:], T.rxa[:, 0:64, :], [c("rxa_pm")], [c("pmi")], [(T.sem.arr_a, ne * n_in)])
+    dma("y", "l_en", T.eni[:], T.rxa[:, 64:128, :], [c("rxa_en")], [c("eni")])
 
-    for k in range(7):
-        if k < 6:
-            lim = 256.0 * 2.0 ** k * SCALE
-            f = lambda k=k, lim=lim: g.vector.tensor_scalar(T.clip[:, k::7], T.low[:, PR - 1::PR], lim, -lim, A.min, A.max)
-        else:
-            f = lambda: g.vector.tensor_copy(T.clip[:, 6::7], T.low[:, PR - 1::PR])
-        op("v", ("clip", 0), f, [c("low")], [c("clip")])
-    op("v", ("dec", 0), lambda: g.vector.tensor_tensor_scan(T.dec[:], T.horn[:], T.clip[:], 0.0, A.mult, A.add), [c("horn"), c("clip")], [c("dec")])
-    l0 = 16 * me
-    mine = T.land[:, l0:l0 + 16]
-    op("v", ("lab", 0), lambda: g.vector.tensor_scalar(mine, T.dec[:, 6::7], 2.0 ** -6 / SCALE, 1024.0, A.mult, A.add), [c("dec")], [c("land", l0, l0 + 16)])
+    def places(r, pieces, pm, plc, seg, flags, between=None):
+        for k, (q, a, b) in enumerate(runs(pieces[0])):
+            gather(q, ("p%d" % k, r), plc, ("win", 0, V), pm, a, b)
+        for k, (q, a, b) in enumerate(runs([("v", n) for n in pieces[1]])):
+            s0, p0, (m, m0) = seg[1] + a, plc[1] + a, flags(a)
+
+            def f(a=a, n=b - a, s0=s0, p0=p0, m=m, m0=m0):
+                init = 0.0 if a == 0 else T[seg[0]][:, s0 - 1:s0]
+                return g.vector.tensor_tensor_scan(T[seg[0]][:, s0:s0 + n], T[m][:, m0:m0 + n], T[plc[0]][:, p0:p0 + n], init, A.add, A.min)
+            if k == 0 and between:
+                between()
+            op("v", ("c%d" % k, r), f, [c(m), c(plc[0], p0, p0 + b - a)] + ([c(seg[0], s0 - 1, s0)] if a else []), [c(seg[0], s0, s0 + b - a)])
+
+    places(0, CFG["pm0"], "pmo0", ("z16", 0), ("z16", V), lambda a: ("ps_t%d" % (a // 1024), a % 1024),
+           lambda: copy("v", None, T.eno0[:], T.eni0[:], [c("eni0")], [c("eno0")]))
+    for b in range(NB):
+        matmul(("oc", 0), T.ps_l1[:, b:b + 1], T.win[:, BLK * b:BLK * b + BLK], T.sel16[:, 0:1], [c("win"), c("sel16")], [c("ps_l1", b, b + 1)])
+    for k, (q, a, b) in enumerate(runs(CFG["own"], BLK)):
+        gather(q, ("g%d%s" % (k, q), 0), ("upd", 0), ("z16", V, V), "eno0", a, b)
+    for b in range(NB):
+        matmul(("ol", 0), T.ps_l0[:, b:128:NB], T.upd[:, BLK * b:BLK * b + BLK], T.sel16[:, 0:8],
+               [c("upd", BLK * b, BLK * b + BLK), c("sel16")], [c("ps_l0", 0, 128)])
+    copy("v", None, T.tx1[:], T.ps_l0[:, 0:128], [c("ps_l0", 0, 128)], [c("tx1")])
+    mine = T.land1[:, lo:lo + 16]
+    a2a(1, lambda q: T.tx1[:, 16 * q:16 * q + 16], mine, T.sem.arr_c, [c("tx1")])
+    a2a(2, lambda q: T.txs[q], T.rxs[me], T.sem.arr_b, [c("txs")])
+    copy("s", None, mine, T.tx1[:, lo:lo + 16], [c("tx1")], [c("land1")])
+    dma("y", "m_1", T.upd[0:128:16, :], T.rxs[:], [c("rxs")], [c("upd")], [(T.sem.arr_b, ne * n_in)])
+    for i in range(16):
+        dma("y", "m_all", T.mask[i:128:16, :], T.rxs[:], [c("rxs")], [c("mask")])
+
+    op("v", None, lambda: g.vector.tensor_scalar(T.roj[:], T.roi[:], 127, None, A.bitwise_and), [c("roi")], [c("roj")])
+    memset(T.rst16[:, 0::ONE], 1.0, c("rst16"))
+    memset(T.rst64[:], 0.0, c("rst64"))
+    copy("v", None, T.roo[:], T.roj[:], [c("roj")], [c("roo")])
+    copy("v", None, T.pmo[:], T.pmi[:], [c("pmi")], [c("pmo")])
+    memset(T.rst64[:, 0::TWO], 1.0, c("rst64"))
+    copy("v", None, T.eno[:], T.eni[:], [c("eni")], [c("eno")])
+    copy("s", None, T.ownc[:], T.ps_l1[:, 0:NB], [c("ps_l1", 0, NB)], [c("ownc")])
+    for k in range(6):
+        o = T.wid[:, 128 * k:128 * k + 128]
+        op("s", ("wid", 0), lambda o=o, k=k: g.scalar.activation(o, T.ident[:], F.Copy, scale=2.0 ** -(k + 1) / SCALE), [c("ident")], [c("wid")])
+    select("lanes", [[0, 8], [0, 2], [-16, 8]], 0)
+    select("sel64", [[-1, 8], [-17, 8]], -1)
+    for b in range(NB):
+        z0 = 16 * TWO * (b + 1) - BLK
+        op("g", ("z64", 0), lambda z0=z0: g.iota(T.z64[:, z0:z0 + BLK], [[0, BLK]], 0, 0, allow_small_or_imprecise_dtypes=True), [], [c("z64")])
+
+    def minimum(key, per, b0, b1, src, r):
+        z, rst, n = "z%d" % per, "rst%d" % per, per * (b1 - b0)
+        op("v", key, lambda: g.vector.tensor_tensor_scan(T[z][:, 16 * per * b0:16 * per * b1:16], T[rst][:, 0:n], src, 0.0, A.add, A.min),
+           [c(rst), r], [c(z, 16 * per * b0, 16 * per * b1)])
+
+    def turn(k, r, per, b0, b1):
+        z = "z%d" % per
+        for b in range(b0, b1):
+            z0 = 16 * per * (b + 1) - BLK
+            transpose(("t%d" % k, r), "ps_t%d" % k, BLK * (b - b0), T[z][:, z0:z0 + BLK], c(z, z0, z0 + BLK))
+
+    def window(k, r, bank, q, a, b):
+        copy(q, ("x%d%s" % (k, q), r), T.win[:, a:b], T[bank][:, 0:b - a], [c(bank, 0, b - a)], [c("win", a, b)])
+
+    arr = [(T.sem.arr_c, ne * n_in)]
+    half = ONE * NB // 2
+    for k, q in enumerate("vs"):
+        gather(q, None, ("ro", 0), ("land1", 0, 128), "roo", half * k, half * k + half, arr)
+    for k in range(2):
+        minimum(None, ONE, 8 * k, 8 * k + 8, T.ro[:, half * k:half * k + half], c("ro", half * k, half * k + half))
+    for k, (q, b0, b1) in enumerate(runs(CFG["x0"])):
+        turn(k, 0, ONE, b0, b1)
+        window(k, 0, "ps_t%d" % k, q, BLK * b0, BLK * b1)
+
+    for r in range(1, R):
+        plan, per = (CFG["last"], ONE) if r == R - 1 else (CFG["spread" if r % 2 else "merge"], TWO)
+        gs, xs = runs(plan["g"], plan["u"]), runs(plan["x"], plan["u"])
+        ns = [(gs[a][1] // BLK, gs[b - 1][2] // BLK) for (q, a, b) in runs([(0, n) for n in plan["n"]])]
+        places(r, CFG["pm"], "pmo", ("plc", 0), ("seg", 0), lambda a: ("upd" if r == 1 else "mask", a))
+        for tok in plan["order"].split():
+            t, k = tok[0], int(tok[1:])
+            bank = "ps_l%d" % (k % 4)
+            if t == "G":
+                q, a, b = gs[k]
+                gather(q, ("g%d%s" % (k, q), r), ("upd", 0), ("seg", 0, V), "eno", a, b)
+            elif t == "B":
+                q, a, b = xs[k]
+                matmul(("b%d" % k, r), T[bank][:, 0:b - a], T.lanes[:], T.upd[:, a:b], [c("lanes"), c("upd", a, b)], [c(bank, 0, b - a)])
+            elif t == "L":
+                b0, b1, sel = gs[k][1] // BLK, gs[k][2] // BLK, "sel%d" % per
+                i = [j for j, (n0, n1) in enumerate(ns) if n0 <= b0 < n1][0]
+                for b in range(b0, b1):
+                    bank, o = "ps_l%d" % i, per * (b - ns[i][0])
+                    matmul(("l%d" % k, r), T[bank][:, o:o + per], T.upd[:, BLK * b:BLK * b + BLK], T[sel][:],
+                           [c("upd", BLK * b, BLK * b + BLK), c(sel)], [c(bank, o, o + per)])
+            elif t == "N":
+                b0, b1 = ns[k]
+                minimum(("n%d" % k, r), per, b0, b1, T[bank][:, 0:per * (b1 - b0)], c(bank, 0, per * (b1 - b0)))
+            elif t == "T":
+                turn(k, r, per, xs[k][1] // BLK, xs[k][2] // BLK)
+            else:
+                window(k, r, bank if r % 2 else "ps_t%d" % k, *xs[k])
+
+    l0 = 32 * me
+    low = T.z16[:, 16 * ONE - 16::16 * ONE]
+    copy("s", None, T.land2[:, l0:l0 + 32:2], low, [c("z16")], [c("land2a")])
+    op("v", None, lambda: g.vector.tensor_tensor(T.land2[:, l0 + 1:l0 + 32:2], low, T.ownc[:], A.is_equal), [c("z16"), c("ownc")], [c("land2b")])
+    out = T.land2[:, l0:l0 + 32]
 
     def bcast():
-        return g.remote_dma_fused([RemoteDMATransfer(dst_ids=[dst(d) for d in peers], dma_engine_mask=sum(1 << e for e in es), remote_sem=T.sem.arr_y,
-                                                     srcs=[mine], dsts=[mine for d in peers])], local_sem=T.sem.sent)
-    op("g", ("none", 1), bcast, [c("land", l0, l0 + 16)], [])
-    arr = [(T.sem.arr_y, len(es) * len(peers))]
-    op("t", ("fin_t", 0), lambda: g.tensor.transpose(T.ps_b0[:, 0:128], T.land[:], T.identf[:]), [c("land", l0, l0 + 16), c("identf")], [c("ps_b0", 0, 128)], 1, arr)
-    op("v", ("fin_e", 0), lambda: g.vector.tensor_tensor(T.eq[:], T.land[:], T.own[:], A.is_equal), [c("land", l0, l0 + 16), c("own")], [c("eq")], 1, arr)
-    copy("s", ("fin_l", 0), T.lab[:], T.ps_b0[:, 0:128], [c("ps_b0", 0, 128)], [c("lab")])
-    for b in range(16):
-        op("t", ("fin_n", 0), lambda b=b: g.tensor.matmul(T.ps_s0[0:8, 0:1], T.eq[:, b::16], T.ones[:, 0:1], b == 0, b == 15), [c("eq"), c("ones")], [c("ps_s0", 0, 1)])
-    copy("v", ("fin_c", 0), T.num[0:8, 0:1], T.ps_s0[0:8, 0:1], [c("ps_s0", 0, 1)], [c("num")])
-    dma("s", "st_y", T.y[:], T.lab[:], [c("lab")], [])
-    dma("y", "st_c", T.cnt[:], T.num[0:8, 0:1], [c("num")], [])
+        tr = RemoteDMATransfer(dst_ids=[dst(d) for d in peers], dma_engine_mask=sum(1 << e for e in es[0:n_all]), remote_sem=T.sem.arr_y,
+                               srcs=[out], dsts=[out for d in peers])
+        return g.remote_dma_fused([tr], local_sem=T.sem.sent)
+    op("g", ("none", 3), bcast, [c("land2a"), c("land2b")], [])
+    arr = [(T.sem.arr_y, n_all * n_in)]
+    for b in range(NB):
+        matmul(("fin_n", 0), T.ps_l1[0:8, 0:1], T.land2[:, 2 * b + 1::32], T.ones[:, 0:1], [c("land2b"), c("ones")], [c("ps_l1", 0, 1)],
+               b == 0, b == NB - 1, arr if b == 0 else [])
+    copy("s", None, T.num[0:8, 0:1], T.ps_l1[0:8, 0:1], [c("ps_l1", 0, 1)], [c("num")])
+    dma("s", "st_c", T.cnt[:], T.num[0:8, 0:1], [c("num")], [])
+    code = T.land2[:, 0::2]
+    matmul(("fin_m", 0), T.ps_l0[:, 0:128], code, T.wid[:, 640:768], [c("land2a"), c("wid")], [c("ps_l0", 0, 128)], True, False)
+    for k in range(6):
+        lim, o = 256.0 * 2.0 ** k * SCALE, T.clip[:, 128 * k:128 * k + 128]
+        op("v", ("clip%d" % (k // 3), 0), lambda lim=lim, o=o: g.vector.tensor_scalar(o, code, lim, -lim, A.min, A.max),
+           [c("land2a")], [c("clip", 128 * k, 128 * k + 128)], 1, arr if k == 0 else [])
+    for k in range(6):
+        matmul(("fin_m", 0), T.ps_l0[:, 0:128], T.clip[:, 128 * k:128 * k + 128], T.wid[:, 128 * k:128 * k + 128],
+               [c("clip", 128 * k, 128 * k + 128), c("wid")], [c("ps_l0", 0, 128)], False, k == 5)
+    op("v", None, lambda: g.vector.tensor_scalar(T.lab[:], T.ps_l0[:, 0:128], 1024.0, None, A.add), [c("ps_l0", 0, 128)], [c("lab")])
+    dma("y", "st_y", T.y[:], T.lab[:], [c("lab")], [])
 
     emit(queues, ops, [T.sem["q%d" % i] for i in range(140)])
-    g.wait_ge(T.sem.sent, 2 * n_in + len(es))
+    g.wait_ge(T.sem.sent, 3 * ne * n_in + n_all)

from concourse.bass import DstId, RemoteDMATransfer
from concourse.mybir import AluOpType as A, ActivationFunctionType as F

V, R, BLK = 2048, 8, 128
NB = V // BLK
ONE, TWO = 16, 64
CFG = {
    "pm": ([("v", 640), ("s", 640), ("s", 608), ("v", 160)], [1280, 768]),
    "pm0": ([("v", 704), ("s", 320), ("s", 928), ("v", 96)], [1024, 1024]),
    "spread": {"u": 32, "g": [("v", 14), ("s", 21), ("v", 15), ("s", 14)], "n": [],
               "x": [("v", 11), ("s", 8), ("v", 16), ("s", 15), ("v", 10), ("s", 4)],
               "order": "G0 G1 G2 G3 B0 X0 B1 X1 B2 X2 B3 X3 B4 X4 B5 X5"},
    "merge": {"u": BLK, "g": [("v", 3), ("s", 5), ("v", 4), ("s", 4)], "n": [1, 1, 1, 1],
              "x": [("s", 2), ("v", 6), ("s", 4), ("v", 4)],
              "order": "G0 G1 G2 G3 L0 L1 N0 L2 T0 N1 L3 N2 X0 N3 T1 T2 X1 T3 X2 X3"},
    "last": {"u": BLK, "g": [("v", 5), ("s", 6), ("v", 2), ("s", 2), ("v", 1)], "n": [1, 2, 2], "x": [],
             "order": "G0 G1 G2 G3 G4 L0 L1 L2 N0 L3 L4 N1 N2"},
    "own": [("v", 6), ("s", 6), ("v", 2), ("s", 2)],
    "x0": [("v", 6), ("s", 4), ("v", 3), ("v", 3)],
    "codes_late": 2, "stt": "v",
    "codes_s": 7,
    "engines": 2,
}
SCALE = 2.0 ** -16

SCRATCH = {
    "txa": ("dram", [8, 128, 32], "int32"), "rxa": ("dram", [8, 128, 32], "int32"),
    "txs": ("dram", [8, 128, 16], "bfloat16"), "rxs": ("dram", [8, 128, 16], "bfloat16"),
    "sti": ("sbuf", [128, 128], "int32"), "stb": ("sbuf", [128, 128], "bfloat16"), "stt": ("sbuf", [128, 144], "bfloat16"),
    "pmi0": ("sbuf", [128, 128], "int32"), "eni0": ("sbuf", [128, 128], "int32"),
    "pmo0": ("sbuf", [128, 128], "uint16"), "eno0": ("sbuf", [128, 128], "uint16"),
    "pmi": ("sbuf", [128, 128], "int32"), "eni": ("sbuf", [128, 128], "int32"),
    "pmo": ("sbuf", [128, 128], "uint16"), "eno": ("sbuf", [128, 128], "uint16"),
    "roi": ("sbuf", [128, 16], "int32"), "roj": ("sbuf", [128, 16], "int32"), "roo": ("sbuf", [128, 16], "uint16"),
    "win": ("sbuf", [128, V], "bfloat16"), "mask": ("sbuf", [128, V], "bfloat16"),
    "plc": ("sbuf", [128, V], "bfloat16"), "seg": ("sbuf", [128, V], "bfloat16"), "upd": ("sbuf", [128, V], "bfloat16"),
    "z16": ("sbuf", [128, 16 * ONE * NB], "bfloat16"), "z64": ("sbuf", [128, 16 * TWO * NB], "bfloat16"),
    "ones": ("sbuf", [128, 128], "bfloat16"), "ident": ("sbuf", [128, 128], "bfloat16"), "ramp": ("sbuf", [128, 128], "bfloat16"),
    "lanes": ("sbuf", [128, 128], "bfloat16"),
    "sel16": ("sbuf", [128, ONE], "bfloat16"), "rst16": ("sbuf", [128, ONE * NB], "bfloat16"),
    "sel64": ("sbuf", [128, TWO], "bfloat16"), "rst64": ("sbuf", [128, TWO * 8], "bfloat16"),
    "tx1": ("sbuf", [128, 128], "bfloat16"), "land1": ("sbuf", [128, 128], "bfloat16"), "ro": ("sbuf", [128, ONE * NB], "bfloat16"),
    "ownc": ("sbuf", [128, NB], "bfloat16"), "land2": ("sbuf", [128, 256], "bfloat16"),
    "wid": ("sbuf", [128, 6 * 128], "bfloat16"), "clip": ("sbuf", [128, 6 * 128], "bfloat16"),
    "lab": ("sbuf", [128, 128], "float32"), "num": ("sbuf", [128, 4], "float32"),
    "ps_l0": ("psum", [128, 512], "float32"), "ps_l1": ("psum", [128, 512], "float32"),
    "ps_l2": ("psum", [128, 512], "float32"), "ps_l3": ("psum", [128, 512], "float32"),
    "ps_t0": ("psum", [128, 1024], "bfloat16"), "ps_t1": ("psum", [128, 1024], "bfloat16"),
    "ps_t2": ("psum", [128, 1024], "bfloat16"), "ps_t3": ("psum", [128, 1024], "bfloat16"),
}
REMOTE = ["arr_a", "arr_b", "arr_c", "arr_y", "sent"]
SEMAPHORES = REMOTE + ["q%d" % i for i in range(140)]


def emit(queues, ops, sems):
    batches = {}
    for i, o in enumerate(ops):
        batches.setdefault(o["key"], []).append(i)
    hist, obs, snap, used, waits = {}, {}, {}, {}, []
    for i, o in enumerate(ops):
        q, deps = o["q"], []
        both = [(0, x) for x in o["r"]] + [(1, x) for x in o["w"]]
        for kind, (b, c0, c1) in both:
            for (j, d0, d1, w) in hist.get(b, []):
                cross = b.startswith("ps_") and ops[j]["q"] != q
                if not cross and (not (kind or w) or d1 <= c0 or c1 <= d0):
                    continue
                if ops[j]["key"] != o["key"]:
                    deps.append(j)
        for kind, (b, c0, c1) in both:
            h = hist.setdefault(b, [])
            if kind and not b.startswith("ps_"):
                h[:] = [x for x in h if not (c0 <= x[1] and x[2] <= c1) or ops[x[0]]["key"] == o["key"]]
            elif kind:
                h[:] = [x for x in h if not (c0 <= x[1] and x[2] <= c1 and ops[x[0]]["q"] == q) or ops[x[0]]["key"] == o["key"]]
                if len(h) > 120:
                    h[:] = h[-120:]
            h.append((i, c0, c1, kind))
        seen = obs.setdefault(q, {})
        need = []
        for j in sorted(set(deps), reverse=True):
            name, b = ops[j]["key"]
            if seen.get(name, -1) >= b:
                continue
            need.append((name, b))
            used[name] = True
            for k in batches[(name, b)]:
                for n2, b2 in snap[k].items():
                    if seen.get(n2, -1) < b2:
                        seen[n2] = b2
            seen[name] = b
        waits.append(need)
        snap[i] = dict(seen)
    keep = {}
    for o in ops:
        n = o["key"][0]
        if (n in used or o["inc"] == 16) and n not in keep:
            keep[n] = sems.pop(0)
    level, total = {}, {}
    for o in ops:
        n, b = o["key"]
        if n in keep:
            total[n] = total.get(n, 0) + o["inc"]
            level[(n, b)] = total[n]
    done = {}
    for i, o in enumerate(ops):
        eng = queues[o["q"]]
        for (s, v) in o["ext"]:
            eng.wait_ge(s, v)
        for kb in waits[i]:
            eng.wait_ge(keep[kb[0]], level[kb])
            done[kb[0]] = max(done.get(kb[0], 0), level[kb])
        ins = o["f"]()
        if o["key"][0] in keep:
            ins.then_inc(keep[o["key"][0]], o["inc"])
    for n in keep:
        if done.get(n, 0) < total[n]:
            queues["y"].wait_ge(keep[n], total[n])


def runs(pieces, unit=1):
    out, a = [], 0
    for q, n in pieces:
        out.append((q, a, a + n * unit))
        a += n * unit
    return out


def rank_program(g, core, T, topo):
    me = T.rank_of(core)
    if me is None:
        return
    cores = list(T.cores)
    peers = [cores[(me + k) % len(cores)] for k in range(1, len(cores))]
    n_in = len(peers)
    queues = {"g": g, "v": g.vector, "s": g.scalar, "t": g.tensor, "y": g.sync}
    ops = []
    uniq = [0]

    def op(q, key, f, r=(), w=(), inc=1, ext=()):
        if key is None:
            uniq[0] += 1
            key = ("u%d" % uniq[0], 0)
        ops.append({"q": q, "key": key, "f": f, "r": list(r), "w": list(w), "inc": inc, "ext": list(ext)})

    def dma(q, key, out, in_, r, w, ext=()):
        op(q, (key, 0), lambda: queues[q].dma_start(out, in_), r, w, 16, ext)

    def c(n, a=0, b=None):
        return (n, a, 8 * V if b is None else b)

    def dst(d):
        rid, pid = topo.addr(d)[0:2]
        return DstId(rid=rid, pnc=pid)

    def copy(q, key, o, i, r, w, ext=()):
        f = (lambda: g.vector.tensor_copy(o, i)) if q == "v" else (lambda: g.scalar.activation(o, i, F.Copy))
        op(q, key, f, r, w, 1, ext)

    def gather(q, key, out, win, off, a, b, ext=()):
        copy(q, key, T[out[0]][:, out[1] + a:out[1] + b], T[win[0]][:, win[1]:win[1] + win[2]].indirect(T[off][:, a // 16:b // 16]),
             [c(win[0], win[1], win[1] + win[2]), c(off)], [c(out[0], out[1] + a, out[1] + b)], ext)

    def matmul(key, out, lhs, rhs, r, w, start=True, stop=True, ext=()):
        op("t", key, lambda: g.tensor.matmul(out, lhs, rhs, start, stop), r, w, 1, ext)

    def transpose(key, bank, o, in_, r):
        op("t", key, lambda: g.tensor.transpose(T[bank][:, o:o + BLK], in_, T.ident[:]), [r, c("ident")], [c(bank, o, o + BLK)])

    def select(name, pattern, base):
        n = T[name].shape[1]
        op("g", None, lambda: g.affine_select(T[name][:], T.ones[:, 0:n], pattern, A.is_equal, 0.0, base, 1), [c("ones")], [c(name)])

    def memset(ap, value, w):
        op("v", None, lambda: g.vector.memset(ap, value), [], [w])

    es, ne = topo.engines(core, peers[0]), CFG["engines"]
    eng = [es[ne * k:ne * k + ne] for k in range(n_in)]
    n_all = ne * (n_in + 1)

    def a2a(n, src, to, arr, r):
        def f():
            tr = [RemoteDMATransfer(dst_ids=[dst(d)], dma_engine_mask=sum(1 << e for e in eng[k]), remote_sem=arr,
                                    srcs=[src(T.rank_of(d))], dsts=[to]) for k, d in enumerate(peers)]
            return g.remote_dma_fused(tr, local_sem=T.sem.sent)
        op("g", ("none", n), f, r, [])

    lo = 16 * me
    dma("s", "n_st", T.sti[:], T.st[:], [], [c("sti")])
    dma("y", "n_pm", T.pmi0[:], T.pm[:], [], [c("pmi0")])
    dma("y", "h_pm", T.txa[:, 0:64, :], T.pm[:], [], [c("txa_pm")])
    dma("y", "h_en", T.txa[:, 64:128, :], T.en[:], [], [c("txa_en")])
    dma("y", "n_en", T.eni0[:], T.en[:], [], [c("eni0")])
    dma("y", "o_pm", T.rxa[me, 0:64, :], T.pm[lo:lo + 16, :], [], [c("rxa_pm")])
    dma("y", "o_en", T.rxa[me, 64:128, :], T.en[lo:lo + 16, :], [], [c("rxa_en")])
    memset(T.ones[:], 1.0, c("ones"))
    memset(T.stt[:, 128:144], 0.0, c("stt", 128, 144))
    memset(T.rst16[:], 0.0, c("rst16"))
    op("g", None, lambda: g.iota(T.ramp[:], [[1, 128]], 0, 0, allow_small_or_imprecise_dtypes=True), [], [c("ramp")])
    select("ident", [[-1, 128]], 0)
    select("sel16", [[0, 2], [-16, 8]], 0)
    op("g", None, lambda: g.iota(T.roi[:], [[1, NB]], 0, NB), [], [c("roi")])
    a2a(0, lambda q: T.txa[q], T.rxa[me], T.sem.arr_a, [c("txa_pm"), c("txa_en")])

    def codes(q, e):
        m = 2.0 ** max((e - 8 if e >= 8 else 7 - e) - 1, 0) * SCALE
        a = 0.0 if e == 8 else (-128.0 if e == 7 else (128.0 if e > 7 else -256.0))
        o = T.win[:, BLK * e:BLK * e + BLK]
        if q == "v":
            f = lambda: g.vector.tensor_scalar(o, T.ramp[:], m, a * m, A.mult, A.add)
        else:
            f = lambda: g.scalar.activation(o, T.ramp[:], F.Copy, bias=a * m, scale=m)
        op(q, ("w0" + q, 0), f, [c("ramp")], [c("win", BLK * e, BLK * e + BLK)])
    late = NB - CFG["codes_late"]
    for e in range(late):
        codes("s" if e < CFG["codes_s"] else "v", e)

    copy("v", None, T.stb[:], T.sti[:], [c("sti")], [c("stb")])
    copy("v", None, T.pmo0[:], T.pmi0[:], [c("pmi0")], [c("pmo0")])
    for e in range(late, NB):
        codes("v", e)
    transpose(None, "ps_t2", 0, T.stb[:], c("stb"))
    copy(CFG["stt"], None, T.stt[:, 0:BLK], T.ps_t2[:, 0:BLK], [c("ps_t2", 0, BLK)], [c("stt", 0, BLK)])
    for b in range(NB):
        transpose(("fl%d" % (b // 8), 0), "ps_t%d" % (b // 8), BLK * (b % 8), T.stt[:, b:b + BLK], c("stt"))
    dma("y", "h_st", T.txs[:], T.stb[:], [c("stb")], [c("txs")])
    dma("y", "o_st", T.rxs[me], T.stb[lo:lo + 16, :], [c("stb")], [c("rxs")])
    dma("y", "l_pm", T.pmi[:], T.rxa[:, 0:64, :], [c("rxa_pm")], [c("pmi")], [(T.sem.arr_a, ne * n_in)])
    dma("y", "l_en", T.eni[:], T.rxa[:, 64:128, :], [c("rxa_en")], [c("eni")])

    def places(r, pieces, pm, plc, seg, flags, between=None):
        for k, (q, a, b) in enumerate(runs(pieces[0])):
            gather(q, ("p%d" % k, r), plc, ("win", 0, V), pm, a, b)
        for k, (q, a, b) in enumerate(runs([("v", n) for n in pieces[1]])):
            s0, p0, (m, m0) = seg[1] + a, plc[1] + a, flags(a)

            def f(a=a, n=b - a, s0=s0, p0=p0, m=m, m0=m0):
                init = 0.0 if a == 0 else T[seg[0]][:, s0 - 1:s0]
                return g.vector.tensor_tensor_scan(T[seg[0]][:, s0:s0 + n], T[m][:, m0:m0 + n], T[plc[0]][:, p0:p0 + n], init, A.add, A.min)
            if k == 0 and between:
                between()
            op("v", ("c%d" % k, r), f, [c(m), c(plc[0], p0, p0 + b - a)] + ([c(seg[0], s0 - 1, s0)] if a else []), [c(seg[0], s0, s0 + b - a)])

    places(0, CFG["pm0"], "pmo0", ("z16", 0), ("z16", V), lambda a: ("ps_t%d" % (a // 1024), a % 1024),
           lambda: copy("v", None, T.eno0[:], T.eni0[:], [c("eni0")], [c("eno0")]))
    for b in range(NB):
        matmul(("oc", 0), T.ps_l1[:, b:b + 1], T.win[:, BLK * b:BLK * b + BLK], T.sel16[:, 0:1], [c("win"), c("sel16")], [c("ps_l1", b, b + 1)])
    for k, (q, a, b) in enumerate(runs(CFG["own"], BLK)):
        gather(q, ("g%d%s" % (k, q), 0), ("upd", 0), ("z16", V, V), "eno0", a, b)
    for b in range(NB):
        matmul(("ol", 0), T.ps_l0[:, b:128:NB], T.upd[:, BLK * b:BLK * b + BLK], T.sel16[:, 0:8],
               [c("upd", BLK * b, BLK * b + BLK), c("sel16")], [c("ps_l0", 0, 128)])
    copy("v", None, T.tx1[:], T.ps_l0[:, 0:128], [c("ps_l0", 0, 128)], [c("tx1")])
    mine = T.land1[:, lo:lo + 16]
    a2a(1, lambda q: T.tx1[:, 16 * q:16 * q + 16], mine, T.sem.arr_c, [c("tx1")])
    a2a(2, lambda q: T.txs[q], T.rxs[me], T.sem.arr_b, [c("txs")])
    copy("s", None, mine, T.tx1[:, lo:lo + 16], [c("tx1")], [c("land1")])
    dma("y", "m_1", T.upd[0:128:16, :], T.rxs[:], [c("rxs")], [c("upd")], [(T.sem.arr_b, ne * n_in)])
    for i in range(16):
        dma("y", "m_all", T.mask[i:128:16, :], T.rxs[:], [c("rxs")], [c("mask")])

    op("v", None, lambda: g.vector.tensor_scalar(T.roj[:], T.roi[:], 127, None, A.bitwise_and), [c("roi")], [c("roj")])
    memset(T.rst16[:, 0::ONE], 1.0, c("rst16"))
    memset(T.rst64[:], 0.0, c("rst64"))
    copy("v", None, T.roo[:], T.roj[:], [c("roj")], [c("roo")])
    copy("v", None, T.pmo[:], T.pmi[:], [c("pmi")], [c("pmo")])
    memset(T.rst64[:, 0::TWO], 1.0, c("rst64"))
    copy("v", None, T.eno[:], T.eni[:], [c("eni")], [c("eno")])
    copy("s", None, T.ownc[:], T.ps_l1[:, 0:NB], [c("ps_l1", 0, NB)], [c("ownc")])
    for k in range(6):
        o = T.wid[:, 128 * k:128 * k + 128]
        op("s", ("wid", 0), lambda o=o, k=k: g.scalar.activation(o, T.ident[:], F.Copy, scale=2.0 ** -(k + 1) / SCALE), [c("ident")], [c("wid")])
    select("lanes", [[0, 8], [0, 2], [-16, 8]], 0)
    select("sel64", [[-1, 8], [-17, 8]], -1)
    for b in range(NB):
        z0 = 16 * TWO * (b + 1) - BLK
        op("g", ("z64", 0), lambda z0=z0: g.iota(T.z64[:, z0:z0 + BLK], [[0, BLK]], 0, 0, allow_small_or_imprecise_dtypes=True), [], [c("z64")])

    def minimum(key, per, b0, b1, src, r):
        z, rst, n = "z%d" % per, "rst%d" % per, per * (b1 - b0)
        op("v", key, lambda: g.vector.tensor_tensor_scan(T[z][:, 16 * per * b0:16 * per * b1:16], T[rst][:, 0:n], src, 0.0, A.add, A.min),
           [c(rst), r], [c(z, 16 * per * b0, 16 * per * b1)])

    def turn(k, r, per, b0, b1):
        z = "z%d" % per
        for b in range(b0, b1):
            z0 = 16 * per * (b + 1) - BLK
            transpose(("t%d" % k, r), "ps_t%d" % k, BLK * (b - b0), T[z][:, z0:z0 + BLK], c(z, z0, z0 + BLK))

    def window(k, r, bank, q, a, b):
        copy(q, ("x%d%s" % (k, q), r), T.win[:, a:b], T[bank][:, 0:b - a], [c(bank, 0, b - a)], [c("win", a, b)])

    arr = [(T.sem.arr_c, ne * n_in)]
    half = ONE * NB // 2
    for k, q in enumerate("vs"):
        gather(q, None, ("ro", 0), ("land1", 0, 128), "roo", half * k, half * k + half, arr)
    for k in range(2):
        minimum(None, ONE, 8 * k, 8 * k + 8, T.ro[:, half * k:half * k + half], c("ro", half * k, half * k + half))
    for k, (q, b0, b1) in enumerate(runs(CFG["x0"])):
        turn(k, 0, ONE, b0, b1)
        window(k, 0, "ps_t%d" % k, q, BLK * b0, BLK * b1)

    for r in range(1, R):
        plan, per = (CFG["last"], ONE) if r == R - 1 else (CFG["spread" if r % 2 else "merge"], TWO)
        gs, xs = runs(plan["g"], plan["u"]), runs(plan["x"], plan["u"])
        ns = [(gs[a][1] // BLK, gs[b - 1][2] // BLK) for (q, a, b) in runs([(0, n) for n in plan["n"]])]
        places(r, CFG["pm"], "pmo", ("plc", 0), ("seg", 0), lambda a: ("upd" if r == 1 else "mask", a))
        for tok in plan["order"].split():
            t, k = tok[0], int(tok[1:])
            bank = "ps_l%d" % (k % 4)
            if t == "G":
                q, a, b = gs[k]
                gather(q, ("g%d%s" % (k, q), r), ("upd", 0), ("seg", 0, V), "eno", a, b)
            elif t == "B":
                q, a, b = xs[k]
                matmul(("b%d" % k, r), T[bank][:, 0:b - a], T.lanes[:], T.upd[:, a:b], [c("lanes"), c("upd", a, b)], [c(bank, 0, b - a)])
            elif t == "L":
                b0, b1, sel = gs[k][1] // BLK, gs[k][2] // BLK, "sel%d" % per
                i = [j for j, (n0, n1) in enumerate(ns) if n0 <= b0 < n1][0]
                for b in range(b0, b1):
                    bank, o = "ps_l%d" % i, per * (b - ns[i][0])
                    matmul(("l%d" % k, r), T[bank][:, o:o + per], T.upd[:, BLK * b:BLK * b + BLK], T[sel][:],
                           [c("upd", BLK * b, BLK * b + BLK), c(sel)], [c(bank, o, o + per)])
            elif t == "N":
                b0, b1 = ns[k]
                minimum(("n%d" % k, r), per, b0, b1, T[bank][:, 0:per * (b1 - b0)], c(bank, 0, per * (b1 - b0)))
            elif t == "T":
                turn(k, r, per, xs[k][1] // BLK, xs[k][2] // BLK)
            else:
                window(k, r, bank if r % 2 else "ps_t%d" % k, *xs[k])

    l0 = 32 * me
    low = T.z16[:, 16 * ONE - 16::16 * ONE]
    copy("s", None, T.land2[:, l0:l0 + 32:2], low, [c("z16")], [c("land2a")])
    op("v", None, lambda: g.vector.tensor_tensor(T.land2[:, l0 + 1:l0 + 32:2], low, T.ownc[:], A.is_equal), [c("z16"), c("ownc")], [c("land2b")])
    out = T.land2[:, l0:l0 + 32]

    def bcast():
        tr = RemoteDMATransfer(dst_ids=[dst(d) for d in peers], dma_engine_mask=sum(1 << e for e in es[0:n_all]), remote_sem=T.sem.arr_y,
                               srcs=[out], dsts=[out for d in peers])
        return g.remote_dma_fused([tr], local_sem=T.sem.sent)
    op("g", ("none", 3), bcast, [c("land2a"), c("land2b")], [])
    arr = [(T.sem.arr_y, n_all * n_in)]
    for b in range(NB):
        matmul(("fin_n", 0), T.ps_l1[0:8, 0:1], T.land2[:, 2 * b + 1::32], T.ones[:, 0:1], [c("land2b"), c("ones")], [c("ps_l1", 0, 1)],
               b == 0, b == NB - 1, arr if b == 0 else [])
    copy("s", None, T.num[0:8, 0:1], T.ps_l1[0:8, 0:1], [c("ps_l1", 0, 1)], [c("num")])
    dma("s", "st_c", T.cnt[:], T.num[0:8, 0:1], [c("num")], [])
    code = T.land2[:, 0::2]
    matmul(("fin_m", 0), T.ps_l0[:, 0:128], code, T.wid[:, 640:768], [c("land2a"), c("wid")], [c("ps_l0", 0, 128)], True, False)
    for k in range(6):
        lim, o = 256.0 * 2.0 ** k * SCALE, T.clip[:, 128 * k:128 * k + 128]
        op("v", ("clip%d" % (k // 3), 0), lambda lim=lim, o=o: g.vector.tensor_scalar(o, code, lim, -lim, A.min, A.max),
           [c("land2a")], [c("clip", 128 * k, 128 * k + 128)], 1, arr if k == 0 else [])
    for k in range(6):
        matmul(("fin_m", 0), T.ps_l0[:, 0:128], T.clip[:, 128 * k:128 * k + 128], T.wid[:, 128 * k:128 * k + 128],
               [c("clip", 128 * k, 128 * k + 128), c("wid")], [c("ps_l0", 0, 128)], False, k == 5)
    op("v", None, lambda: g.vector.tensor_scalar(T.lab[:], T.ps_l0[:, 0:128], 1024.0, None, A.add), [c("ps_l0", 0, 128)], [c("lab")])
    dma("y", "st_y", T.y[:], T.lab[:], [c("lab")], [])

    emit(queues, ops, [T.sem["q%d" % i] for i in range(140)])
    g.wait_ge(T.sem.sent, 3 * ne * n_in + n_all)
